import numpy as np
import ml_dtypes


def mxq(x, axis, fmt="e4m3"):
    dtype, down = {"e4m3": (ml_dtypes.float8_e4m3fn, 7), "e5m2": (ml_dtypes.float8_e5m2, 14)}[fmt]
    v = np.moveaxis(np.asarray(x, np.float32).astype(ml_dtypes.bfloat16).astype(np.float64), axis, -1)
    blocks = v.reshape(v.shape[:-1] + (-1, 32))
    amax = np.abs(blocks).max(-1, keepdims=True)
    byte = np.maximum(np.where(amax > 0, np.frexp(amax)[1] - 1 + 127, 0) - down, 1)
    scale = np.exp2(byte - 127.0)
    codes = (blocks / scale).astype(np.float32).astype(dtype).astype(np.float64)
    return np.moveaxis((codes * scale).reshape(v.shape), -1, axis)


WIDE = False


def mx_kscale(k):
    if not WIDE:
        return np.ones(k)
    levels = np.array([30, -30])
    if k % 512:
        return np.exp2(np.random.permutation(np.resize(levels, k // 32))).repeat(32)
    a = np.empty((k // 512, 16))
    for p in range(k // 512):
        a[p, :8] = np.random.permutation(np.resize(levels, 8))
        for g in range(8):
            far = levels[np.abs(levels - a[p, g]) >= 10]
            a[p, g + 8] = far[np.random.randint(len(far))]
    return np.exp2(a.ravel()).repeat(32)


def f64(x):
    return np.asarray(x).astype(np.float64)


def striped(idx):
    return np.tile(idx.reshape(-1, 16).T, (8, 1)).astype(np.uint16)


def unstriped(offs):
    return offs[:16].T.reshape(-1).astype(np.int64)


def silu(v):
    return v / (1.0 + np.exp(-np.maximum(v, -700.0)))


def d_silu(v):
    s = 1.0 / (1.0 + np.exp(-np.maximum(v, -700.0)))
    return s * (1.0 + v * (1.0 - s))


K, T, E, C, H, N = 128, 1024, 4, 512, 512, 512


def by_expert(wq, xq):
    return np.concatenate([wq[e].T @ xq[:, e * C:(e + 1) * C] for e in range(E)], axis=1)


def setup_inputs():
    n = np.random.standard_normal
    s = mx_kscale(N)[:, None]
    u = mx_kscale(H)
    first = np.random.permutation(np.repeat(np.arange(E), T // E))
    second = (first + 1 + np.random.permutation(np.repeat(np.arange(E - 1), -(-T // (E - 1)))[:T])) % E
    while np.bincount(second, minlength=E).max() != T // E:
        load = np.bincount(second, minlength=E); hi, lo = int(load.argmax()), int(load.argmin())
        t = np.flatnonzero((second == hi) & (first != lo))[0]; second[t] = lo
    slot_token = np.empty(E * C, np.int64); pos = np.empty((2, T), np.int64); fill = np.zeros(E, np.int64)
    place = np.stack([np.random.permutation(C) for _ in range(E)])
    for r, deal in enumerate((first, second)):
        for t in np.random.permutation(T):
            e = deal[t]; j = e * C + place[e, fill[e]]; fill[e] += 1; slot_token[j] = t; pos[r, t] = j
    g = np.random.uniform(0.2, 0.8, T)
    w_slot = np.empty(E * C); w_slot[pos[0]] = g; w_slot[pos[1]] = 1.0 - g
    return {
        "dyT": (n((N, T)) * s).astype(np.float32),
        "a1": n((H, E * C)).astype(np.float32),
        "a3": n((H, E * C)).astype(np.float32),
        "w2": (n((E, N, H)) / np.sqrt(N) / s[None] * u[None, None, :]).astype(np.float32),
        "w1": (n((E, H, K)) / np.sqrt(H) / u[None, :, None]).astype(np.float32),
        "w3": (n((E, H, K)) / np.sqrt(H) / u[None, :, None]).astype(np.float32),
        "gate": np.tile(w_slot, (N, 1)).astype(np.float32),
        "offs": striped(slot_token),
        "pos1": striped(pos[0]),
        "pos2": striped(pos[1]),
    }


def reference(dyT, a1, a3, w2, w1, w3, gate, offs, pos1, pos2):
    idx = unstriped(offs)
    gq = mxq(f64(gate) * f64(dyT)[:, idx], 0, "e5m2")
    dh = by_expert(mxq(f64(w2), 1, "e4m3"), gq)
    da1 = dh * f64(a3) * d_silu(f64(a1))
    da3 = dh * silu(f64(a1))
    dx = by_expert(mxq(f64(w1), 1, "e4m3"), mxq(da1, 0, "e5m2")) + by_expert(mxq(f64(w3), 1, "e4m3"), mxq(da3, 0, "e5m2"))
    return dx[:, unstriped(pos1)] + dx[:, unstriped(pos2)]

@@ -1,0 +1,243 @@
+from contextlib import ExitStack
+
+import concourse.mybir as mybir
+
+K, T, E, C, H, N = 128, 1024, 4, 512, 512, 512
+S = E * C
+P = 128
+PACK = 4
+
+FLOPS = 2 * S * H * N + 2 * 2 * S * H * K
+BYTES = 4 * (N * T + 2 * H * S + S + E * N * H + 2 * E * H * K + K * T) + 2 * P * (S + 2 * T) // 16
+
+F32 = mybir.dt.float32
+BF16 = mybir.dt.bfloat16
+U32 = mybir.dt.uint32
+U16 = mybir.dt.uint16
+U8 = mybir.dt.uint8
+E4M3X4 = mybir.dt.float8_e4m3fn_x4
+E5M2X4 = mybir.dt.float8_e5m2_x4
+
+ADD = mybir.AluOpType.add
+SUB = mybir.AluOpType.subtract
+MULT = mybir.AluOpType.mult
+SIGMOID = mybir.ActivationFunctionType.Sigmoid
+SILU = mybir.ActivationFunctionType.Silu
+
+
+def tile_moe_bdx_glu_silu_kernel(tc, dyT, a1, a3, w2, w1, w3, gate, offs, pos1, pos2, out):
+    nc = tc.nc
+    with ExitStack() as ctx:
+        held = ctx.enter_context(tc.tile_pool(name="held", bufs=1))
+        work = ctx.enter_context(tc.tile_pool(name="work", bufs=2))
+        psum = ctx.enter_context(tc.psum_pool(name="psum", bufs=2))
+
+        offs_sb = held.tile([P, S // 16], U16, name="offs_sb")
+        pos1_sb = held.tile([P, T // 16], U16, name="pos1_sb")
+        pos2_sb = held.tile([P, T // 16], U16, name="pos2_sb")
+        dy_sb = [held.tile([P, T], F32, name="dy%d" % t) for t in range(PACK)]
+        gate_sb = [held.tile([P, C], F32, name="gate%d" % e) for e in range(E)]
+        a1_sb = [held.tile([P, PACK, C], F32, name="a1_%d" % e) for e in range(E)]
+        f_sb = [held.tile([P, PACK, C], F32, name="f_%d" % e) for e in range(E)]
+        dx_sb = held.tile([P, S], F32, name="dx_sb")
+        warm = held.tile([P, 1], F32, name="warm")
+        warm_out = held.tile([P, 1], F32, name="warm_out")
+
+        nc.vector.memset(warm[:], 0.0)
+        nc.scalar.activation(warm_out[:], warm[:], SIGMOID)
+
+        def load_gate(e):
+            nc.sync.dma_start(out=gate_sb[e][:], in_=gate[0:P, e * C : (e + 1) * C])
+
+        def load_w2(e):
+            raw = work.tile([P, PACK, H], F32, name="w2_raw", tag="w2_raw", bufs=2)
+            nc.sync.dma_start(out=raw[:], in_=w2[e].rearrange("(p t) i -> p t i", t=PACK))
+            return raw
+
+        def load_w13(e):
+            raw = work.tile([P, 2, C], F32, name="w13_raw", tag="w13_raw", bufs=2)
+            nc.sync.dma_start(out=raw[:, 0, :], in_=w1[e].rearrange("(q r) k -> q (r k)", r=PACK))
+            nc.sync.dma_start(out=raw[:, 1, :], in_=w3[e].rearrange("(q r) k -> q (r k)", r=PACK))
+            return raw
+
+        def load_a1(e):
+            nc.sync.dma_start(out=a1_sb[e][:], in_=a1[:, e * C : (e + 1) * C].rearrange("(q r) s -> q r s", r=PACK))
+
+        def load_a3(e):
+            raw = work.tile([P, PACK, C], F32, name="a3_raw", tag="a3_raw", bufs=2)
+            nc.sync.dma_start(out=raw[:], in_=a3[:, e * C : (e + 1) * C].rearrange("(q r) s -> q r s", r=PACK))
+            return raw
+
+        nc.sync.dma_start(offs_sb[:], offs)
+        load_gate(0)
+        dy_rows = dyT.rearrange("(p t) c -> p t c", t=PACK)
+        for t in range(PACK):
+            nc.sync.dma_start(out=dy_sb[t][:], in_=dy_rows[:, t, :])
+        for e in range(1, E):
+            load_gate(e)
+        w2_raw, w13_raw, a3_raw = {}, {}, {}
+        w2_raw[0] = load_w2(0)
+        for e in range(E):
+            load_a1(e)
+        a3_raw[0] = load_a3(0)
+        w13_raw[0] = load_w13(0)
+        w2_raw[1] = load_w2(1)
+        a3_raw[1] = load_a3(1)
+        w13_raw[1] = load_w13(1)
+
+        g_raw, g_grp, g_mx, w2_grp, w2_mx, w13_mx, dh_sb, da_mx = {}, {}, {}, {}, {}, {}, {}, {}
+
+        def gather(e):
+            g = work.tile([P, PACK, C], F32, name="g_raw", tag="g_raw", bufs=3)
+            cols = offs_sb[:, e * C // 16 : (e + 1) * C // 16]
+            for t in range(PACK):
+                nc.vector.tensor_tensor(g[:, t, :], dy_sb[t][:].indirect(cols), gate_sb[e][:], MULT)
+            g_raw[e] = g
+
+        def group_g(e):
+            grp = work.tile([P, C * PACK], BF16, name="g_grp", tag="g_grp", bufs=2, align_bytes=64)
+            nc.scalar.copy(
+                out=grp[:].rearrange("p (c i t) -> p c t i", i=4, t=PACK),
+                in_=g_raw[e][:].rearrange("p t (c i) -> p c t i", i=4),
+            )
+            g_grp[e] = grp
+
+        def group_w2(e):
+            grp = work.tile([P, H * PACK], BF16, name="w2_grp", tag="w2_grp", bufs=2, align_bytes=64)
+            nc.scalar.copy(
+                out=grp[:].rearrange("p (r q t) -> p q t r", r=PACK, t=PACK),
+                in_=w2_raw[e][:].rearrange("p t (q r) -> p q t r", r=PACK),
+            )
+            w2_grp[e] = grp
+
+        def group_w13(e):
+            grp = work.tile([P, 2 * K * PACK], BF16, name="w13_grp", tag="w13_grp", bufs=2, align_bytes=64)
+            for m in range(2):
+                nc.scalar.copy(
+                    out=grp[:, m * K * PACK : (m + 1) * K * PACK].rearrange("p (c i r) -> p c r i", i=4, r=PACK),
+                    in_=w13_raw[e][:, m, :].rearrange("p (r c i) -> p c r i", i=4, r=PACK),
+                )
+            return grp
+
+        def quantise(grp, tag, bufs, fmt, width):
+            codes = work.tile([P, width], U32, name=tag + "_codes", tag=tag + "_codes", bufs=bufs, align_bytes=64)
+            scales = work.tile([P, width], U8, name=tag + "_scales", tag=tag + "_scales", bufs=bufs, align_bytes=64)
+            nc.vector.quantize_mx(out=codes[:].bitcast(fmt), scales=scales[:], in_=grp[:])
+            return codes, scales
+
+        def first_product(e):
+            gc, gs = g_mx[e]
+            wc, ws = w2_mx[e]
+            banks = []
+            for r in range(PACK):
+                bank = psum.tile([P, C], F32, name="dh", tag="dh", bufs=6)
+                cols = slice(r * P, (r + 1) * P)
+                nc.tensor.matmul_mx(
+                    out=bank[:],
+                    lhsT=wc[:, cols].bitcast(E4M3X4),
+                    lhsT_scale=ws[:, cols],
+                    rhs=gc[:].bitcast(E5M2X4),
+                    rhs_scale=gs[:],
+                    start=True,
+                    stop=True,
+                )
+                banks.append(bank)
+            return banks
+
+        def empty_dh(e, banks):
+            dh = work.tile([P, PACK, C], F32, name="dh_sb", tag="dh_sb", bufs=2)
+            for r in range(PACK):
+                nc.scalar.copy(out=dh[:, r, :], in_=banks[r][:])
+            dh_sb[e] = dh
+
+        def derivative(e):
+            f, h = f_sb[e], a1_sb[e]
+            nc.vector.scalar_tensor_tensor(out=f[:], in0=h[:], scalar=1.0, in1=f[:], op0=SUB, op1=MULT)
+
+        def times_a3(e):
+            f = f_sb[e]
+            nc.vector.scalar_tensor_tensor(out=f[:], in0=f[:], scalar=1.0, in1=a3_raw[e][:], op0=ADD, op1=MULT)
+
+        def make_da(e, factor):
+            grp = work.tile([P, C * PACK], BF16, name="da_grp", tag="da_grp", bufs=3, align_bytes=64)
+            nc.vector.tensor_tensor(
+                grp[:].rearrange("p (c i r) -> p c r i", i=4, r=PACK),
+                dh_sb[e][:].rearrange("p r (c i) -> p c r i", i=4),
+                factor[:].rearrange("p r (c i) -> p c r i", i=4),
+                MULT,
+            )
+            return grp
+
+        def second_product(e, da1, da3):
+            wc, ws = w13_mx[e]
+            bank = psum.tile([P, C], F32, name="dx", tag="dx", bufs=2)
+            for m, (codes, scales) in enumerate((da1, da3)):
+                cols = slice(m * K, (m + 1) * K)
+                nc.tensor.matmul_mx(
+                    out=bank[:],
+                    lhsT=wc[:, cols].bitcast(E4M3X4),
+                    lhsT_scale=ws[:, cols],
+                    rhs=codes[:].bitcast(E5M2X4),
+                    rhs_scale=scales[:],
+                    start=m == 0,
+                    stop=m == 1,
+                )
+            nc.scalar.copy(out=dx_sb[:, e * C : (e + 1) * C], in_=bank[:])
+
+        gather(0)
+        group_g(0)
+        group_w2(0)
+        gather(1)
+        for e in range(E):
+            nc.scalar.activation(f_sb[e][:], a1_sb[e][:], SIGMOID, scale=-1.0)
+        gather(2)
+        gather(3)
+        w2_mx[0] = quantise(w2_grp[0], "w2", 2, E4M3X4, H)
+        g_mx[0] = quantise(g_grp[0], "g", 2, E5M2X4, C)
+        banks = first_product(0)
+        nc.scalar.activation(a1_sb[0][:], a1_sb[0][:], SILU)
+        empty_dh(0, banks)
+        derivative(0)
+        nc.scalar.activation(a1_sb[1][:], a1_sb[1][:], SILU)
+        times_a3(0)
+        for e in range(E):
+            if e + 1 < E:
+                group_g(e + 1)
+                group_w2(e + 1)
+            w13_grp = group_w13(e)
+            if e + 2 < E:
+                w2_raw[e + 2] = load_w2(e + 2)
+                a3_raw[e + 2] = load_a3(e + 2)
+            da1_grp = make_da(e, f_sb[e])
+            if e + 1 < E:
+                w2_mx[e + 1] = quantise(w2_grp[e + 1], "w2", 2, E4M3X4, H)
+                g_mx[e + 1] = quantise(g_grp[e + 1], "g", 2, E5M2X4, C)
+                banks = first_product(e + 1)
+            w13_mx[e] = quantise(w13_grp, "w13", 2, E4M3X4, 2 * K)
+            if e + 2 < E:
+                w13_raw[e + 2] = load_w13(e + 2)
+            if e == 0:
+                nc.sync.dma_start(pos1_sb[:], pos1)
+                nc.sync.dma_start(pos2_sb[:], pos2)
+            da3_grp = make_da(e, a1_sb[e])
+            if e + 1 < E:
+                empty_dh(e + 1, banks)
+            da1 = quantise(da1_grp, "da1", 2, E5M2X4, C)
+            if e + 1 < E:
+                derivative(e + 1)
+            if e + 2 < E:
+                nc.scalar.activation(a1_sb[e + 2][:], a1_sb[e + 2][:], SILU)
+            da3 = quantise(da3_grp, "da3", 2, E5M2X4, C)
+            second_product(e, da1, da3)
+            if e + 1 < E:
+                times_a3(e + 1)
+
+        start = 0
+        for piece in (512, 256, 256):
+            cols = slice(start // 16, (start + piece) // 16)
+            pair = work.tile([P, 2, piece], F32, name="pair", tag="pair", bufs=2)
+            nc.vector.tensor_copy(pair[:, 0, :], dx_sb[:].indirect(pos1_sb[:, cols]))
+            nc.vector.tensor_copy(pair[:, 1, :], dx_sb[:].indirect(pos2_sb[:, cols]))
+            nc.vector.tensor_tensor(pair[:, 0, :], pair[:, 0, :], pair[:, 1, :], ADD)
+            nc.sync.dma_start(out=out[:, start : start + piece], in_=pair[:, 0, :])
+            start += piece

@@ -22,6 +22,7 @@ ADD = mybir.AluOpType.add
 SUB = mybir.AluOpType.subtract
 MULT = mybir.AluOpType.mult
 SIGMOID = mybir.ActivationFunctionType.Sigmoid
+COPY = mybir.ActivationFunctionType.Copy
 SILU = mybir.ActivationFunctionType.Silu
 
 
@@ -40,6 +41,8 @@ def tile_moe_bdx_glu_silu_kernel(tc, dyT, a1, a3, w2, w1, w3, gate, offs, pos1, 
         a1_sb = [held.tile([P, PACK, C], F32, name="a1_%d" % e) for e in range(E)]
         f_sb = [held.tile([P, PACK, C], F32, name="f_%d" % e) for e in range(E)]
         dx_sb = held.tile([P, S], F32, name="dx_sb")
+        fin = held.tile([P, 2, T], F32, name="fin")
+        pin = held.tile([P, 4], F32, name="pin")
         warm = held.tile([P, 1], F32, name="warm")
         warm_out = held.tile([P, 1], F32, name="warm_out")
 
@@ -73,15 +76,18 @@ def tile_moe_bdx_glu_silu_kernel(tc, dyT, a1, a3, w2, w1, w3, gate, offs, pos1, 
         dy_rows = dyT.rearrange("(p t) c -> p t c", t=PACK)
         for t in range(PACK):
             nc.sync.dma_start(out=dy_sb[t][:], in_=dy_rows[:, t, :])
-        for e in range(1, E):
-            load_gate(e)
         w2_raw, w13_raw, a3_raw = {}, {}, {}
+        load_gate(1)
         w2_raw[0] = load_w2(0)
-        for e in range(E):
-            load_a1(e)
+        load_a1(0)
+        load_gate(2)
+        load_a1(1)
+        load_gate(3)
         a3_raw[0] = load_a3(0)
-        w13_raw[0] = load_w13(0)
         w2_raw[1] = load_w2(1)
+        w13_raw[0] = load_w13(0)
+        load_a1(2)
+        load_a1(3)
         a3_raw[1] = load_a3(1)
         w13_raw[1] = load_w13(1)
 
@@ -152,11 +158,26 @@ def tile_moe_bdx_glu_silu_kernel(tc, dyT, a1, a3, w2, w1, w3, gate, offs, pos1, 
 
         def derivative(e):
             f, h = f_sb[e], a1_sb[e]
-            nc.vector.scalar_tensor_tensor(out=f[:], in0=h[:], scalar=1.0, in1=f[:], op0=SUB, op1=MULT)
+            for r in (0, 2):
+                nc.vector.scalar_tensor_tensor(
+                    out=f[:, r : r + 2, :], in0=h[:, r : r + 2, :], scalar=1.0, in1=f[:, r : r + 2, :], op0=SUB, op1=MULT
+                )
+            for r in (0, 2):
+                nc.vector.scalar_tensor_tensor(
+                    out=f[:, r : r + 2, :], in0=f[:, r : r + 2, :], scalar=1.0, in1=a3_raw[e][:, r : r + 2, :], op0=ADD, op1=MULT
+                )
 
-        def times_a3(e):
-            f = f_sb[e]
-            nc.vector.scalar_tensor_tensor(out=f[:], in0=f[:], scalar=1.0, in1=a3_raw[e][:], op0=ADD, op1=MULT)
+        def sigmoids(e0, e1, bias):
+            for e in range(e0, e1):
+                nc.scalar.activation(f_sb[e][:], a1_sb[e][:], SIGMOID, scale=-1.0, bias=bias)
+
+        def silus(e, bias):
+            for r in (0, 2):
+                nc.scalar.activation(a1_sb[e][:, r : r + 2, :], a1_sb[e][:, r : r + 2, :], SILU, bias=bias)
+
+        def pin_order(j, src):
+            nc.scalar.activation(pin[:, j : j + 1], src, COPY, scale=0.0)
+            return pin[:, j : j + 1]
 
         def make_da(e, factor):
             grp = work.tile([P, C * PACK], BF16, name="da_grp", tag="da_grp", bufs=3, align_bytes=64)
@@ -187,57 +208,63 @@ def tile_moe_bdx_glu_silu_kernel(tc, dyT, a1, a3, w2, w1, w3, gate, offs, pos1, 
         gather(0)
         group_g(0)
         group_w2(0)
+        sigmoids(0, 2, 0.0)
+        after_n1 = pin_order(0, f_sb[1][:, 0, 0:1])
         gather(1)
-        for e in range(E):
-            nc.scalar.activation(f_sb[e][:], a1_sb[e][:], SIGMOID, scale=-1.0)
-        gather(2)
-        gather(3)
         w2_mx[0] = quantise(w2_grp[0], "w2", 2, E4M3X4, H)
         g_mx[0] = quantise(g_grp[0], "g", 2, E5M2X4, C)
         banks = first_product(0)
-        nc.scalar.activation(a1_sb[0][:], a1_sb[0][:], SILU)
+        silus(0, after_n1)
         empty_dh(0, banks)
         derivative(0)
-        nc.scalar.activation(a1_sb[1][:], a1_sb[1][:], SILU)
-        times_a3(0)
+        silus(1, after_n1)
+        after_h1 = pin_order(1, a1_sb[1][:, 3, 0:1])
         for e in range(E):
             if e + 1 < E:
                 group_g(e + 1)
                 group_w2(e + 1)
             w13_grp = group_w13(e)
+            if e == 0:
+                sigmoids(2, 4, after_h1)
+                after_n3 = pin_order(2, f_sb[3][:, 0, 0:1])
             if e + 2 < E:
+                gather(e + 2)
                 w2_raw[e + 2] = load_w2(e + 2)
                 a3_raw[e + 2] = load_a3(e + 2)
             da1_grp = make_da(e, f_sb[e])
+            da3_grp = make_da(e, a1_sb[e])
             if e + 1 < E:
                 w2_mx[e + 1] = quantise(w2_grp[e + 1], "w2", 2, E4M3X4, H)
                 g_mx[e + 1] = quantise(g_grp[e + 1], "g", 2, E5M2X4, C)
                 banks = first_product(e + 1)
+                empty_dh(e + 1, banks)
             w13_mx[e] = quantise(w13_grp, "w13", 2, E4M3X4, 2 * K)
             if e + 2 < E:
                 w13_raw[e + 2] = load_w13(e + 2)
             if e == 0:
                 nc.sync.dma_start(pos1_sb[:], pos1)
                 nc.sync.dma_start(pos2_sb[:], pos2)
-            da3_grp = make_da(e, a1_sb[e])
-            if e + 1 < E:
-                empty_dh(e + 1, banks)
             da1 = quantise(da1_grp, "da1", 2, E5M2X4, C)
-            if e + 1 < E:
-                derivative(e + 1)
-            if e + 2 < E:
-                nc.scalar.activation(a1_sb[e + 2][:], a1_sb[e + 2][:], SILU)
             da3 = quantise(da3_grp, "da3", 2, E5M2X4, C)
             second_product(e, da1, da3)
+            if e + 2 < E:
+                silus(e + 2, after_n3)
             if e + 1 < E:
-                times_a3(e + 1)
+                derivative(e + 1)
 
-        start = 0
-        for piece in (512, 256, 256):
-            cols = slice(start // 16, (start + piece) // 16)
-            pair = work.tile([P, 2, piece], F32, name="pair", tag="pair", bufs=2)
-            nc.vector.tensor_copy(pair[:, 0, :], dx_sb[:].indirect(pos1_sb[:, cols]))
-            nc.vector.tensor_copy(pair[:, 1, :], dx_sb[:].indirect(pos2_sb[:, cols]))
-            nc.vector.tensor_tensor(pair[:, 0, :], pair[:, 0, :], pair[:, 1, :], ADD)
-            nc.sync.dma_start(out=out[:, start : start + piece], in_=pair[:, 0, :])
-            start += piece
+        ends = (0, 512, 768, 1024)
+        pieces = list(zip(ends, ends[1:]))
+
+        def fetch(j, slot_list, a, b):
+            nc.vector.tensor_copy(fin[:, j, a:b], dx_sb[:].indirect(slot_list[:, a // 16 : b // 16]))
+
+        def add_and_store(a, b):
+            nc.vector.tensor_tensor(fin[:, 0, a:b], fin[:, 0, a:b], fin[:, 1, a:b], ADD)
+            nc.sync.dma_start(out=out[:, a:b], in_=fin[:, 0, a:b])
+
+        for i, (a, b) in enumerate(pieces):
+            fetch(0, pos1_sb, a, b)
+            if i > 0:
+                add_and_store(*pieces[i - 1])
+            fetch(1, pos2_sb, a, b)
+        add_and_store(*pieces[-1])

@@ -125,10 +125,16 @@ def tile_moe_bdx_glu_silu_kernel(tc, dyT, a1, a3, w2, w1, w3, gate, offs, pos1, 
                 )
             return grp
 
-        def quantise(grp, tag, bufs, fmt, width):
+        def quantise(grp, tag, bufs, fmt, width, parts=1):
             codes = work.tile([P, width], U32, name=tag + "_codes", tag=tag + "_codes", bufs=bufs, align_bytes=64)
             scales = work.tile([P, width], U8, name=tag + "_scales", tag=tag + "_scales", bufs=bufs, align_bytes=64)
-            nc.vector.quantize_mx(out=codes[:].bitcast(fmt), scales=scales[:], in_=grp[:])
+            step = width // parts
+            for a in range(0, width, step):
+                nc.vector.quantize_mx(
+                    out=codes[:, a : a + step].bitcast(fmt),
+                    scales=scales[:, a : a + step],
+                    in_=grp[:, a * PACK : (a + step) * PACK],
+                )
             return codes, scales
 
         def first_product(e):
@@ -156,15 +162,20 @@ def tile_moe_bdx_glu_silu_kernel(tc, dyT, a1, a3, w2, w1, w3, gate, offs, pos1, 
                 nc.scalar.copy(out=dh[:, r, :], in_=banks[r][:])
             dh_sb[e] = dh
 
-        def derivative(e):
+        def derivative(e, step):
             f, h = f_sb[e], a1_sb[e]
-            for r in (0, 2):
+            for r in range(0, PACK, step):
+                rows = slice(r, r + step)
                 nc.vector.scalar_tensor_tensor(
-                    out=f[:, r : r + 2, :], in0=h[:, r : r + 2, :], scalar=1.0, in1=f[:, r : r + 2, :], op0=SUB, op1=MULT
+                    out=f[:, rows, :], in0=h[:, rows, :], scalar=1.0, in1=f[:, rows, :], op0=SUB, op1=MULT
                 )
-            for r in (0, 2):
+
+        def times_a3(e, step):
+            f = f_sb[e]
+            for r in range(0, PACK, step):
+                rows = slice(r, r + step)
                 nc.vector.scalar_tensor_tensor(
-                    out=f[:, r : r + 2, :], in0=f[:, r : r + 2, :], scalar=1.0, in1=a3_raw[e][:, r : r + 2, :], op0=ADD, op1=MULT
+                    out=f[:, rows, :], in0=f[:, rows, :], scalar=1.0, in1=a3_raw[e][:, rows, :], op0=ADD, op1=MULT
                 )
 
         def sigmoids(e0, e1, bias):
@@ -179,27 +190,27 @@ def tile_moe_bdx_glu_silu_kernel(tc, dyT, a1, a3, w2, w1, w3, gate, offs, pos1, 
             nc.scalar.activation(pin[:, j : j + 1], src, COPY, scale=0.0)
             return pin[:, j : j + 1]
 
-        def make_da(e, factor):
-            grp = work.tile([P, C * PACK], BF16, name="da_grp", tag="da_grp", bufs=3, align_bytes=64)
+        def make_da(e, factor, grp):
             nc.vector.tensor_tensor(
-                grp[:].rearrange("p (c i r) -> p c r i", i=4, r=PACK),
+                grp.rearrange("p (c i r) -> p c r i", i=4, r=PACK),
                 dh_sb[e][:].rearrange("p r (c i) -> p c r i", i=4),
                 factor[:].rearrange("p r (c i) -> p c r i", i=4),
                 MULT,
             )
-            return grp
 
-        def second_product(e, da1, da3):
+        def second_product(e, da):
             wc, ws = w13_mx[e]
             bank = psum.tile([P, C], F32, name="dx", tag="dx", bufs=2)
-            for m, (codes, scales) in enumerate((da1, da3)):
+            codes, scales = da
+            for m in range(2):
                 cols = slice(m * K, (m + 1) * K)
+                slots = slice(m * C, (m + 1) * C)
                 nc.tensor.matmul_mx(
                     out=bank[:],
                     lhsT=wc[:, cols].bitcast(E4M3X4),
                     lhsT_scale=ws[:, cols],
-                    rhs=codes[:].bitcast(E5M2X4),
-                    rhs_scale=scales[:],
+                    rhs=codes[:, slots].bitcast(E5M2X4),
+                    rhs_scale=scales[:, slots],
                     start=m == 0,
                     stop=m == 1,
                 )
@@ -216,7 +227,8 @@ def tile_moe_bdx_glu_silu_kernel(tc, dyT, a1, a3, w2, w1, w3, gate, offs, pos1, 
         banks = first_product(0)
         silus(0, after_n1)
         empty_dh(0, banks)
-        derivative(0)
+        derivative(0, 2)
+        times_a3(0, 2)
         silus(1, after_n1)
         after_h1 = pin_order(1, a1_sb[1][:, 3, 0:1])
         for e in range(E):
@@ -224,33 +236,34 @@ def tile_moe_bdx_glu_silu_kernel(tc, dyT, a1, a3, w2, w1, w3, gate, offs, pos1, 
                 group_g(e + 1)
                 group_w2(e + 1)
             w13_grp = group_w13(e)
-            if e == 0:
-                sigmoids(2, 4, after_h1)
-                after_n3 = pin_order(2, f_sb[3][:, 0, 0:1])
             if e + 2 < E:
                 gather(e + 2)
                 w2_raw[e + 2] = load_w2(e + 2)
                 a3_raw[e + 2] = load_a3(e + 2)
-            da1_grp = make_da(e, f_sb[e])
-            da3_grp = make_da(e, a1_sb[e])
+            da_grp = work.tile([P, 2 * C * PACK], BF16, name="da_grp", tag="da_grp", bufs=1, align_bytes=64)
+            make_da(e, f_sb[e], da_grp[:, : C * PACK])
+            make_da(e, a1_sb[e], da_grp[:, C * PACK :])
             if e + 1 < E:
                 w2_mx[e + 1] = quantise(w2_grp[e + 1], "w2", 2, E4M3X4, H)
                 g_mx[e + 1] = quantise(g_grp[e + 1], "g", 2, E5M2X4, C)
                 banks = first_product(e + 1)
                 empty_dh(e + 1, banks)
+            if e == 0:
+                sigmoids(2, 4, after_h1)
+                after_n3 = pin_order(2, f_sb[3][:, 0, 0:1])
             w13_mx[e] = quantise(w13_grp, "w13", 2, E4M3X4, 2 * K)
             if e + 2 < E:
                 w13_raw[e + 2] = load_w13(e + 2)
             if e == 0:
                 nc.sync.dma_start(pos1_sb[:], pos1)
                 nc.sync.dma_start(pos2_sb[:], pos2)
-            da1 = quantise(da1_grp, "da1", 2, E5M2X4, C)
-            da3 = quantise(da3_grp, "da3", 2, E5M2X4, C)
-            second_product(e, da1, da3)
+            if e + 1 < E:
+                derivative(e + 1, PACK)
+            second_product(e, quantise(da_grp, "da", 2, E5M2X4, 2 * C, parts=1 if e + 1 < E else 2))
             if e + 2 < E:
                 silus(e + 2, after_n3)
             if e + 1 < E:
-                derivative(e + 1)
+                times_a3(e + 1, PACK)
 
         ends = (0, 512, 768, 1024)
         pieces = list(zip(ends, ends[1:]))
@@ -258,13 +271,13 @@ def tile_moe_bdx_glu_silu_kernel(tc, dyT, a1, a3, w2, w1, w3, gate, offs, pos1, 
         def fetch(j, slot_list, a, b):
             nc.vector.tensor_copy(fin[:, j, a:b], dx_sb[:].indirect(slot_list[:, a // 16 : b // 16]))
 
-        def add_and_store(a, b):
-            nc.vector.tensor_tensor(fin[:, 0, a:b], fin[:, 0, a:b], fin[:, 1, a:b], ADD)
+        def add_and_store(engine, a, b):
+            engine.tensor_tensor(fin[:, 0, a:b], fin[:, 0, a:b], fin[:, 1, a:b], ADD)
             nc.sync.dma_start(out=out[:, a:b], in_=fin[:, 0, a:b])
 
         for i, (a, b) in enumerate(pieces):
             fetch(0, pos1_sb, a, b)
             if i > 0:
-                add_and_store(*pieces[i - 1])
+                add_and_store(nc.gpsimd, *pieces[i - 1])
             fetch(1, pos2_sb, a, b)
-        add_and_store(*pieces[-1])
+        add_and_store(nc.vector, *pieces[-1])

from contextlib import ExitStack

import concourse.mybir as mybir

K, T, E, C, H, N = 128, 1024, 4, 512, 512, 512
S = E * C
P = 128
PACK = 4

FLOPS = 2 * S * H * N + 2 * 2 * S * H * K
BYTES = 4 * (N * T + 2 * H * S + S + E * N * H + 2 * E * H * K + K * T) + 2 * P * (S + 2 * T) // 16

F32 = mybir.dt.float32
BF16 = mybir.dt.bfloat16
U32 = mybir.dt.uint32
U16 = mybir.dt.uint16
U8 = mybir.dt.uint8
E4M3X4 = mybir.dt.float8_e4m3fn_x4
E5M2X4 = mybir.dt.float8_e5m2_x4

ADD = mybir.AluOpType.add
SUB = mybir.AluOpType.subtract
MULT = mybir.AluOpType.mult
SIGMOID = mybir.ActivationFunctionType.Sigmoid
COPY = mybir.ActivationFunctionType.Copy
SILU = mybir.ActivationFunctionType.Silu


def tile_moe_bdx_glu_silu_kernel(tc, dyT, a1, a3, w2, w1, w3, gate, offs, pos1, pos2, out):
    nc = tc.nc
    with ExitStack() as ctx:
        held = ctx.enter_context(tc.tile_pool(name="held", bufs=1))
        work = ctx.enter_context(tc.tile_pool(name="work", bufs=2))
        psum = ctx.enter_context(tc.psum_pool(name="psum", bufs=2))

        offs_sb = held.tile([P, S // 16], U16, name="offs_sb")
        pos1_sb = held.tile([P, T // 16], U16, name="pos1_sb")
        pos2_sb = held.tile([P, T // 16], U16, name="pos2_sb")
        dy_sb = [held.tile([P, T], F32, name="dy%d" % t) for t in range(PACK)]
        gate_sb = [held.tile([P, C], F32, name="gate%d" % e) for e in range(E)]
        a1_sb = [held.tile([P, PACK, C], F32, name="a1_%d" % e) for e in range(E)]
        f_sb = [held.tile([P, PACK, C], F32, name="f_%d" % e) for e in range(E)]
        dx_sb = held.tile([P, S], F32, name="dx_sb")
        fin = held.tile([P, 2, T], F32, name="fin")
        pin = held.tile([P, 4], F32, name="pin")
        warm = held.tile([P, 1], F32, name="warm")
        warm_out = held.tile([P, 1], F32, name="warm_out")

        nc.vector.memset(warm[:], 0.0)
        nc.scalar.activation(warm_out[:], warm[:], SIGMOID)

        def load_gate(e):
            nc.sync.dma_start(out=gate_sb[e][:], in_=gate[0:P, e * C : (e + 1) * C])

        def load_w2(e):
            raw = work.tile([P, PACK, H], F32, name="w2_raw", tag="w2_raw", bufs=2)
            nc.sync.dma_start(out=raw[:], in_=w2[e].rearrange("(p t) i -> p t i", t=PACK))
            return raw

        def load_w13(e):
            raw = work.tile([P, 2, C], F32, name="w13_raw", tag="w13_raw", bufs=2)
            nc.sync.dma_start(out=raw[:, 0, :], in_=w1[e].rearrange("(q r) k -> q (r k)", r=PACK))
            nc.sync.dma_start(out=raw[:, 1, :], in_=w3[e].rearrange("(q r) k -> q (r k)", r=PACK))
            return raw

        def load_a1(e):
            nc.sync.dma_start(out=a1_sb[e][:], in_=a1[:, e * C : (e + 1) * C].rearrange("(q r) s -> q r s", r=PACK))

        def load_a3(e):
            raw = work.tile([P, PACK, C], F32, name="a3_raw", tag="a3_raw", bufs=2)
            nc.sync.dma_start(out=raw[:], in_=a3[:, e * C : (e + 1) * C].rearrange("(q r) s -> q r s", r=PACK))
            return raw

        nc.sync.dma_start(offs_sb[:], offs)
        load_gate(0)
        dy_rows = dyT.rearrange("(p t) c -> p t c", t=PACK)
        for t in range(PACK):
            nc.sync.dma_start(out=dy_sb[t][:], in_=dy_rows[:, t, :])
        w2_raw, w13_raw, a3_raw = {}, {}, {}
        load_gate(1)
        w2_raw[0] = load_w2(0)
        load_a1(0)
        load_gate(2)
        load_a1(1)
        load_gate(3)
        a3_raw[0] = load_a3(0)
        w2_raw[1] = load_w2(1)
        w13_raw[0] = load_w13(0)
        load_a1(2)
        load_a1(3)
        a3_raw[1] = load_a3(1)
        w13_raw[1] = load_w13(1)

        g_raw, g_grp, g_mx, w2_grp, w2_mx, w13_mx, dh_sb, da_mx = {}, {}, {}, {}, {}, {}, {}, {}

        def gather(e):
            g = work.tile([P, PACK, C], F32, name="g_raw", tag="g_raw", bufs=3)
            cols = offs_sb[:, e * C // 16 : (e + 1) * C // 16]
            for t in range(PACK):
                nc.vector.tensor_tensor(g[:, t, :], dy_sb[t][:].indirect(cols), gate_sb[e][:], MULT)
            g_raw[e] = g

        def group_g(e):
            grp = work.tile([P, C * PACK], BF16, name="g_grp", tag="g_grp", bufs=2, align_bytes=64)
            nc.scalar.copy(
                out=grp[:].rearrange("p (c i t) -> p c t i", i=4, t=PACK),
                in_=g_raw[e][:].rearrange("p t (c i) -> p c t i", i=4),
            )
            g_grp[e] = grp

        def group_w2(e):
            grp = work.tile([P, H * PACK], BF16, name="w2_grp", tag="w2_grp", bufs=2, align_bytes=64)
            nc.scalar.copy(
                out=grp[:].rearrange("p (r q t) -> p q t r", r=PACK, t=PACK),
                in_=w2_raw[e][:].rearrange("p t (q r) -> p q t r", r=PACK),
            )
            w2_grp[e] = grp

        def group_w13(e):
            grp = work.tile([P, 2 * K * PACK], BF16, name="w13_grp", tag="w13_grp", bufs=2, align_bytes=64)
            for m in range(2):
                nc.scalar.copy(
                    out=grp[:, m * K * PACK : (m + 1) * K * PACK].rearrange("p (c i r) -> p c r i", i=4, r=PACK),
                    in_=w13_raw[e][:, m, :].rearrange("p (r c i) -> p c r i", i=4, r=PACK),
                )
            return grp

        def quantise(grp, tag, bufs, fmt, width, parts=1):
            codes = work.tile([P, width], U32, name=tag + "_codes", tag=tag + "_codes", bufs=bufs, align_bytes=64)
            scales = work.tile([P, width], U8, name=tag + "_scales", tag=tag + "_scales", bufs=bufs, align_bytes=64)
            step = width // parts
            for a in range(0, width, step):
                nc.vector.quantize_mx(
                    out=codes[:, a : a + step].bitcast(fmt),
                    scales=scales[:, a : a + step],
                    in_=grp[:, a * PACK : (a + step) * PACK],
                )
            return codes, scales

        def first_product(e):
            gc, gs = g_mx[e]
            wc, ws = w2_mx[e]
            banks = []
            for r in range(PACK):
                bank = psum.tile([P, C], F32, name="dh", tag="dh", bufs=6)
                cols = slice(r * P, (r + 1) * P)
                nc.tensor.matmul_mx(
                    out=bank[:],
                    lhsT=wc[:, cols].bitcast(E4M3X4),
                    lhsT_scale=ws[:, cols],
                    rhs=gc[:].bitcast(E5M2X4),
                    rhs_scale=gs[:],
                    start=True,
                    stop=True,
                )
                banks.append(bank)
            return banks

        def empty_dh(e, banks):
            dh = work.tile([P, PACK, C], F32, name="dh_sb", tag="dh_sb", bufs=2)
            for r in range(PACK):
                nc.scalar.copy(out=dh[:, r, :], in_=banks[r][:])
            dh_sb[e] = dh

        def derivative(e, step):
            f, h = f_sb[e], a1_sb[e]
            for r in range(0, PACK, step):
                rows = slice(r, r + step)
                nc.vector.scalar_tensor_tensor(
                    out=f[:, rows, :], in0=h[:, rows, :], scalar=1.0, in1=f[:, rows, :], op0=SUB, op1=MULT
                )

        def times_a3(e, step):
            f = f_sb[e]
            for r in range(0, PACK, step):
                rows = slice(r, r + step)
                nc.vector.scalar_tensor_tensor(
                    out=f[:, rows, :], in0=f[:, rows, :], scalar=1.0, in1=a3_raw[e][:, rows, :], op0=ADD, op1=MULT
                )

        def sigmoids(e0, e1, bias):
            for e in range(e0, e1):
                nc.scalar.activation(f_sb[e][:], a1_sb[e][:], SIGMOID, scale=-1.0, bias=bias)

        def silus(e, bias):
            for r in (0, 2):
                nc.scalar.activation(a1_sb[e][:, r : r + 2, :], a1_sb[e][:, r : r + 2, :], SILU, bias=bias)

        def pin_order(j, src):
            nc.scalar.activation(pin[:, j : j + 1], src, COPY, scale=0.0)
            return pin[:, j : j + 1]

        def make_da(e, factor, grp):
            nc.vector.tensor_tensor(
                grp.rearrange("p (c i r) -> p c r i", i=4, r=PACK),
                dh_sb[e][:].rearrange("p r (c i) -> p c r i", i=4),
                factor[:].rearrange("p r (c i) -> p c r i", i=4),
                MULT,
            )

        def second_product(e, da):
            wc, ws = w13_mx[e]
            bank = psum.tile([P, C], F32, name="dx", tag="dx", bufs=2)
            codes, scales = da
            for m in range(2):
                cols = slice(m * K, (m + 1) * K)
                slots = slice(m * C, (m + 1) * C)
                nc.tensor.matmul_mx(
                    out=bank[:],
                    lhsT=wc[:, cols].bitcast(E4M3X4),
                    lhsT_scale=ws[:, cols],
                    rhs=codes[:, slots].bitcast(E5M2X4),
                    rhs_scale=scales[:, slots],
                    start=m == 0,
                    stop=m == 1,
                )
            nc.scalar.copy(out=dx_sb[:, e * C : (e + 1) * C], in_=bank[:])

        gather(0)
        group_g(0)
        group_w2(0)
        sigmoids(0, 2, 0.0)
        after_n1 = pin_order(0, f_sb[1][:, 0, 0:1])
        gather(1)
        w2_mx[0] = quantise(w2_grp[0], "w2", 2, E4M3X4, H)
        g_mx[0] = quantise(g_grp[0], "g", 2, E5M2X4, C)
        banks = first_product(0)
        silus(0, after_n1)
        empty_dh(0, banks)
        derivative(0, 2)
        times_a3(0, 2)
        silus(1, after_n1)
        after_h1 = pin_order(1, a1_sb[1][:, 3, 0:1])
        for e in range(E):
            if e + 1 < E:
                group_g(e + 1)
                group_w2(e + 1)
            w13_grp = group_w13(e)
            if e + 2 < E:
                gather(e + 2)
                w2_raw[e + 2] = load_w2(e + 2)
                a3_raw[e + 2] = load_a3(e + 2)
            da_grp = work.tile([P, 2 * C * PACK], BF16, name="da_grp", tag="da_grp", bufs=1, align_bytes=64)
            make_da(e, f_sb[e], da_grp[:, : C * PACK])
            make_da(e, a1_sb[e], da_grp[:, C * PACK :])
            if e + 1 < E:
                w2_mx[e + 1] = quantise(w2_grp[e + 1], "w2", 2, E4M3X4, H)
                g_mx[e + 1] = quantise(g_grp[e + 1], "g", 2, E5M2X4, C)
                banks = first_product(e + 1)
                empty_dh(e + 1, banks)
            if e == 0:
                sigmoids(2, 4, after_h1)
                after_n3 = pin_order(2, f_sb[3][:, 0, 0:1])
            w13_mx[e] = quantise(w13_grp, "w13", 2, E4M3X4, 2 * K)
            if e + 2 < E:
                w13_raw[e + 2] = load_w13(e + 2)
            if e == 0:
                nc.sync.dma_start(pos1_sb[:], pos1)
                nc.sync.dma_start(pos2_sb[:], pos2)
            if e + 1 < E:
                derivative(e + 1, PACK)
            second_product(e, quantise(da_grp, "da", 2, E5M2X4, 2 * C, parts=1 if e + 1 < E else 2))
            if e + 2 < E:
                silus(e + 2, after_n3)
            if e + 1 < E:
                times_a3(e + 1, PACK)

        ends = (0, 512, 768, 1024)
        pieces = list(zip(ends, ends[1:]))

        def fetch(j, slot_list, a, b):
            nc.vector.tensor_copy(fin[:, j, a:b], dx_sb[:].indirect(slot_list[:, a // 16 : b // 16]))

        def add_and_store(engine, a, b):
            engine.tensor_tensor(fin[:, 0, a:b], fin[:, 0, a:b], fin[:, 1, a:b], ADD)
            nc.sync.dma_start(out=out[:, a:b], in_=fin[:, 0, a:b])

        for i, (a, b) in enumerate(pieces):
            fetch(0, pos1_sb, a, b)
            if i > 0:
                add_and_store(nc.gpsimd, *pieces[i - 1])
            fetch(1, pos2_sb, a, b)
        add_and_store(nc.vector, *pieces[-1])
